import numpy as np
import ml_dtypes


def mxq(x, axis, fmt="e4m3"):
    dtype, down = {"e4m3": (ml_dtypes.float8_e4m3fn, 7), "e5m2": (ml_dtypes.float8_e5m2, 14)}[fmt]
    v = np.moveaxis(np.asarray(x, np.float32).astype(ml_dtypes.bfloat16).astype(np.float64), axis, -1)
    blocks = v.reshape(v.shape[:-1] + (-1, 32))
    amax = np.abs(blocks).max(-1, keepdims=True)
    byte = np.maximum(np.where(amax > 0, np.frexp(amax)[1] - 1 + 127, 0) - down, 1)
    scale = np.exp2(byte - 127.0)
    codes = (blocks / scale).astype(np.float32).astype(dtype).astype(np.float64)
    return np.moveaxis((codes * scale).reshape(v.shape), -1, axis)


WIDE = False


def mx_kscale(k):
    if not WIDE:
        return np.ones(k)
    levels = np.array([10, -10, 5, -5, 0])
    if k % 512:
        return np.exp2(np.random.permutation(np.resize(levels, k // 32))).repeat(32)
    a = np.empty((k // 512, 16))
    for p in range(k // 512):
        a[p, :8] = np.random.permutation(np.resize(levels, 8))
        for g in range(8):
            far = levels[np.abs(levels - a[p, g]) >= 10]
            a[p, g + 8] = far[np.random.randint(len(far))]
    return np.exp2(a.ravel()).repeat(32)


def f64(x):
    return np.asarray(x).astype(np.float64)


def striped(idx):
    return np.tile(idx.reshape(-1, 16).T, (8, 1)).astype(np.uint16)


def unstriped(offs):
    return offs[:16].T.reshape(-1).astype(np.int64)


E2M1 = np.array([0.0, 0.5, 1.0, 1.5, 2.0, 3.0, 4.0, 6.0, -0.0, -0.5, -1.0, -1.5, -2.0, -3.0, -4.0, -6.0])


def pack_weight(w, fmt):
    k, n = w.shape
    w = f64(np.asarray(w, np.float32).astype(ml_dtypes.bfloat16)).reshape(k // 32, 32, n)
    amax = np.abs(w).max(1)
    if fmt == "e4m3":
        byte = np.frexp(amax)[1] - 1 + 127 - 7
    else:
        mant, ex = np.frexp(amax / 6.0)
        byte = np.where(mant > 0.5, ex, ex - 1) + 127
    byte = np.clip(np.where(amax > 0, byte, 1), 1, 254)
    scaled = (w * np.exp2(127.0 - byte)[:, None, :]).reshape(k, n).astype(np.float32)
    by_word = np.ascontiguousarray(scaled.reshape(k // 512, 128, 4, n).transpose(0, 1, 3, 2))
    if fmt == "e4m3":
        words = by_word.astype(ml_dtypes.float8_e4m3fn).view(np.uint8)
    else:
        c = by_word.astype(ml_dtypes.float4_e2m1fn).view(np.uint8) & 0xF
        words = (c[..., 0::2] | (c[..., 1::2] << 4)).reshape(k // 512, 128, 2 * n)
    return np.ascontiguousarray(words), np.ascontiguousarray(byte.astype(np.uint8).reshape(k // 512, 16, n))


def unpack_weight(words, scales, fmt):
    g, _, n = scales.shape
    words = np.ascontiguousarray(words).reshape(g, 128, n, -1)
    if fmt == "e4m3":
        vals = words.view(ml_dtypes.float8_e4m3fn).astype(np.float64)
    else:
        nib = np.empty((g, 128, n, 4), np.uint8)
        nib[..., 0::2] = words & 0xF
        nib[..., 1::2] = words >> 4
        vals = E2M1[nib]
    vals = vals * np.repeat(np.exp2(scales.astype(np.float64) - 127.0), 8, axis=1)[..., None]
    return vals.transpose(0, 1, 3, 2).reshape(g * 512, n)


K, T, E, C, N = 2048, 1280, 8, 256, 128
TOP = 4
PAD = 64


def by_expert(wq, xq):
    return np.concatenate([wq[e].T @ xq[:, e * C:(e + 1) * C] for e in range(E)], axis=1)


def setup_inputs():
    n = np.random.standard_normal
    s = mx_kscale(K)[:, None]
    slot_token = np.empty(E * C, np.int64); pos = np.tile(E * C + np.arange(T) % PAD, (TOP, 1)); taken = np.zeros(T, np.int64)
    liked = np.random.randn(T)
    for e in np.random.permutation(E):
        free = np.flatnonzero(taken < TOP); pick = np.random.permutation(free[np.argsort(-(liked[free] + np.random.gumbel(size=free.size)))[:C]]); slot_token[e * C:(e + 1) * C] = pick
        pos[taken[pick], pick] = e * C + np.arange(C); taken[pick] += 1
    g = np.random.uniform(0.2, 0.8, (TOP, T))
    w = [pack_weight(m, "e2m1") for m in n((E, K, N)) / np.sqrt(K) / s[None]]
    return {
        "xT": (n((K, T)) * s).astype(np.float32),
        "w_words": np.stack([m[0] for m in w]),
        "w_scales": np.stack([m[1] for m in w]),
        "gate": np.stack([np.tile(r, (N, 1)) for r in g]).astype(np.float32),
        "offs": striped(slot_token),
        "pos1": striped(pos[0]),
        "pos2": striped(pos[1]),
        "pos3": striped(pos[2]),
        "pos4": striped(pos[3]),
    }


def reference(xT, w_words, w_scales, gate, offs, pos1, pos2, pos3, pos4):
    idx = unstriped(offs)
    w = np.stack([unpack_weight(w_words[e], w_scales[e], "e2m1") for e in range(E)])
    xq = mxq(f64(xT)[:, idx], 0, "e4m3")
    y = by_expert(w, xq)
    y = np.concatenate([y, np.zeros((N, PAD))], axis=1)
    return sum(f64(gate[r]) * y[:, unstriped(p)] for r, p in enumerate((pos1, pos2, pos3, pos4)))

@@ -1,0 +1,227 @@
+from contextlib import ExitStack
+
+import concourse.mybir as mybir
+from concourse.masks import make_identity
+
+K, T, E, C, N = 2048, 1280, 8, 256, 128
+TOP, PAD = 4, 64
+S = E * C
+P = 128
+PASSES = K // 512
+
+F32 = mybir.dt.float32
+BF16 = mybir.dt.bfloat16
+I32 = mybir.dt.int32
+U32 = mybir.dt.uint32
+U16 = mybir.dt.uint16
+U8 = mybir.dt.uint8
+FP8X4 = mybir.dt.float8_e4m3fn_x4
+FP4X4 = mybir.dt.float4_e2m1fn_x4
+COPY = mybir.ActivationFunctionType.Copy
+
+FLOPS = 2 * K * S * N
+BYTES = K * T * 4 + E * K * N // 2 + E * K * N // 32 + TOP * T * 4 + (S + TOP * T) * 16 + N * T * 4
+
+LOAD_CHUNKS = ((0, 512), (512, 512), (1024, 256))
+HALVES = ((0, 1024), (1024, 1024))
+PIECES = ((0, 768), (768, 768), (1536, 512))
+LAST_PIECES = ((0, 512), (512, 512), (1024, 512), (1536, 512))
+WINDOW = 1408
+BANKS = ((0, 512), (512, 512), (1024, 512), (1536, 256), (1792, 256))
+OUT_CHUNKS = ((0, 512), (512, 384), (896, 384))
+SHIFT_ROWS = 112
+
+
+def tile_moe_ecr_lin_none_kernel(
+    tc, xT, w_words, w_scales, gate, offs, pos1, pos2, pos3, pos4, out
+):
+    nc = tc.nc
+    with ExitStack() as ctx:
+        keep = ctx.enter_context(tc.tile_pool(name="keep", bufs=1))
+        ring = ctx.enter_context(tc.tile_pool(name="ring", bufs=4))
+        psum = ctx.enter_context(tc.psum_pool(name="psum", bufs=8))
+
+        def bank_tile(name):
+            return psum.tile([P, 512], F32, name=name, tag="bank")
+
+        offs_t = keep.tile([P, S // 16], U16, name="offs_t")
+        pos_t = [keep.tile([P, T // 16], U16, name="pos_t%d" % r) for r in range(TOP)]
+        raw = {}
+        grouped = {}
+        for a in range(PASSES):
+            for t0, n in LOAD_CHUNKS:
+                raw[a, t0] = keep.tile([P, 4, n], F32, name="raw", tag="raw%d_%d" % (a, t0))
+                grouped[a, t0] = keep.tile([P, n, 4], BF16, name="grp%d_%d" % (a, t0), align_bytes=64)
+        words = [keep.tile([P, T], U32, name="words%d" % a, align_bytes=64) for a in range(PASSES)]
+        packed = keep.tile([P, WINDOW], U8, name="packed", tag="order", align_bytes=64)
+        slot_words = [keep.tile([P, S], U32, name="slotw%d" % a, align_bytes=64) for a in range(PASSES - 1)]
+        planes = {}
+        for s0, n in HALVES:
+            for a in range(PASSES):
+                planes[a, s0] = keep.tile([P, n], U8, name="plane%d_%d" % (a, s0), align_bytes=64)
+        w_t = [keep.tile([P, E, 2 * N], U8, name="w%d" % a, align_bytes=64) for a in range(PASSES)]
+        wsc = keep.tile([P, E * PASSES, N], U8, name="wsc", align_bytes=64)
+        gate_rows = keep.tile([P, TOP, P], F32, name="gate_rows")
+        ident = keep.tile([P, P], F32, name="ident")
+        y = keep.tile([P, S + PAD], F32, name="y")
+
+        nc.vector.memset(gate_rows[:], 0.0)
+        nc.vector.memset(packed[:].bitcast(I32), 0)
+        nc.vector.memset(wsc[:].bitcast(I32), 0)
+        for s0, n in HALVES:
+            for a in range(1, PASSES):
+                nc.vector.memset(planes[a, s0][:].bitcast(I32), 0)
+        nc.vector.memset(y[:, S:], 0.0)
+        make_identity(nc, ident[:])
+
+        scale_rows = w_scales.rearrange("e a (q r) n -> r q (e a) n", r=4)
+        for a in range(PASSES):
+            rows = xT[512 * a : 512 * (a + 1), :].rearrange("(p j) t -> p j t", j=4)
+            for t0, n in LOAD_CHUNKS:
+                nc.sync.dma_start(out=raw[a, t0][:], in_=rows[:, :, t0 : t0 + n])
+            if a == 0:
+                nc.sync.dma_start(offs_t[:], offs)
+            if a == 1:
+                nc.sync.dma_start(
+                    out=gate_rows[0 : T // P], in_=gate[:, 0, :].rearrange("r (b c) -> b r c", c=P)
+                )
+                for tile, lst in zip(pos_t, (pos1, pos2, pos3, pos4)):
+                    nc.sync.dma_start(tile[:], lst)
+            if a == 2:
+                for r in range(4):
+                    nc.sync.dma_start(out=wsc[r:P:32].bitcast(I32), in_=scale_rows[r].bitcast(I32))
+        for a in range(PASSES):
+            nc.sync.dma_start(
+                out=w_t[a][:].bitcast(I32),
+                in_=w_words[:, a].rearrange("e p c -> p e c").bitcast(I32),
+            )
+
+        def weave(a, t0, lo, hi, on_vector):
+            dst = grouped[a, t0][:, lo:hi, :].rearrange("p (c i) t -> p c t i", i=4)
+            src = raw[a, t0][:, :, lo:hi].rearrange("p t (c i) -> p c t i", i=4)
+            if on_vector:
+                nc.vector.tensor_copy(dst, src)
+            else:
+                nc.scalar.activation(dst, src, COPY)
+
+        def gather_words(a, s0, n):
+            nc.vector.tensor_copy(
+                slot_words[a][:, s0 : s0 + n],
+                words[a][:].indirect(offs_t[:, s0 // 16 : (s0 + n) // 16]),
+            )
+
+        for a in range(PASSES):
+            for t0, n in LOAD_CHUNKS:
+                if a == 0:
+                    cut = n * 5 // 8
+                    weave(a, t0, 0, cut, True)
+                    weave(a, t0, cut, n, False)
+                else:
+                    weave(a, t0, 0, n, False)
+                nc.vector.quantize_mx(
+                    out=words[a][:, t0 : t0 + n].bitcast(FP8X4),
+                    scales=packed[4 * a : P, t0 : t0 + n],
+                    in_=grouped[a, t0][:].rearrange("p w j -> p (w j)"),
+                )
+            if a < PASSES - 1:
+                for s0, n in PIECES:
+                    gather_words(a, s0, n)
+
+        gate_cols = keep.tile(
+            [P, TOP, T // P], F32, name="gate_cols", tag="raw%d_%d" % (PASSES - 1, LOAD_CHUNKS[-1][0])
+        )
+        gbank = bank_tile("gbank")
+        for r in range(TOP):
+            nc.tensor.transpose(gbank[:, r * P : (r + 1) * P], gate_rows[:, r, :], ident[:])
+        nc.scalar.activation(
+            gate_cols[:], gbank[:].rearrange("p (r c) -> p r c", c=P)[:, :, 0 : T // P], COPY
+        )
+
+        for s0, n in HALVES:
+            nc.vector.tensor_copy(
+                planes[0, s0][:], packed[:].indirect(offs_t[:, s0 // 16 : (s0 + n) // 16])
+            )
+            for a in range(1, PASSES):
+                nc.sync.dma_start(
+                    out=planes[a, s0][0:SHIFT_ROWS].bitcast(I32),
+                    in_=planes[0, s0][4 * a : 4 * a + SHIFT_ROWS].bitcast(I32),
+                )
+        slot_words.append(keep.tile([P, S], U32, name="slotw_last", tag="order", align_bytes=64))
+        for s0, n in LAST_PIECES:
+            gather_words(PASSES - 1, s0, n)
+
+        acc = [bank_tile("acc%d" % i) for i in range(len(BANKS))]
+        for h0, hn in HALVES:
+            for a in range(PASSES):
+                for i, (b0, bn) in enumerate(BANKS):
+                    if not h0 <= b0 < h0 + hn:
+                        continue
+                    for s0 in range(b0, b0 + bn, P):
+                        e = s0 // C
+                        nc.tensor.matmul_mx(
+                            out=acc[i][:, s0 - b0 : s0 - b0 + P],
+                            lhsT=w_t[a][:, e, :].bitcast(FP4X4),
+                            lhsT_scale=wsc[:, e * PASSES + a, :],
+                            rhs=slot_words[a][:, s0 : s0 + P].bitcast(FP8X4),
+                            rhs_scale=planes[a, h0][:, s0 - h0 : s0 - h0 + P],
+                            start=(a == 0 and s0 == b0),
+                            stop=(a == PASSES - 1 and s0 + P == b0 + bn),
+                        )
+        for i, (b0, bn) in enumerate(BANKS):
+            if i == len(BANKS) - 1:
+                nc.vector.tensor_copy(y[:, b0 : b0 + bn], acc[i][:, 0:bn])
+            else:
+                nc.scalar.activation(y[:, b0 : b0 + bn], acc[i][:, 0:bn], COPY)
+
+        def scale_block(dst, src, r, g, on_vector):
+            factor = gate_cols[:, r, g : g + 1]
+            if on_vector:
+                nc.vector.tensor_scalar_mul(dst, src, factor)
+            else:
+                nc.scalar.activation(dst, src, COPY, scale=factor)
+
+        for t0, n in OUT_CHUNKS:
+            last_chunk = t0 + n == T
+            blocks = n // P
+            if last_chunk:
+                totals = [bank_tile("total")[:, 0:P] for b in range(blocks)]
+            else:
+                total = bank_tile("total")
+                totals = [total[:, b * P : (b + 1) * P] for b in range(blocks)]
+            for r in range(TOP):
+                very_last = last_chunk and r == TOP - 1
+                picked = ring.tile([P, n], F32, name="picked")
+                nc.vector.tensor_copy(
+                    picked[:], y[:].indirect(pos_t[r][:, t0 // 16 : (t0 + n) // 16])
+                )
+                if very_last:
+                    turned = [bank_tile("turned")[:, 0:P] for b in range(blocks)]
+                else:
+                    one = bank_tile("turned")
+                    turned = [one[:, b * P : (b + 1) * P] for b in range(blocks)]
+                scaled = ring.tile([P, n], F32, name="scaled")
+                for b in range(blocks):
+                    nc.tensor.transpose(turned[b], picked[:, b * P : (b + 1) * P], ident[:])
+                for b in range(blocks):
+                    scale_block(
+                        scaled[:, b * P : (b + 1) * P], turned[b], r, t0 // P + b, very_last and b == 1
+                    )
+                for b in range(blocks):
+                    nc.tensor.matmul(
+                        totals[b],
+                        scaled[:, b * P : (b + 1) * P],
+                        ident[:],
+                        is_transpose=True,
+                        start=(r == 0 and (b == 0 or last_chunk)),
+                        stop=(r == TOP - 1 and (b == blocks - 1 or last_chunk)),
+                    )
+            staged = ring.tile([P, n], F32, name="staged")
+            if last_chunk:
+                for b in range(blocks):
+                    if b == 1:
+                        nc.scalar.activation(staged[:, b * P : (b + 1) * P], totals[b], COPY)
+                    else:
+                        nc.vector.tensor_copy(staged[:, b * P : (b + 1) * P], totals[b])
+            else:
+                nc.scalar.activation(staged[:], total[:, 0:n], COPY)
+            nc.sync.dma_start(out=out[:, t0 : t0 + n], in_=staged[:])

@@ -30,6 +30,7 @@ WINDOW = 1408
 BANKS = ((0, 512), (512, 512), (1024, 512), (1536, 256), (1792, 256))
 OUT_CHUNKS = ((0, 512), (512, 384), (896, 384))
 SHIFT_ROWS = 112
+TURNED = TOP - 1
 
 
 def tile_moe_ecr_lin_none_kernel(
@@ -39,10 +40,10 @@ def tile_moe_ecr_lin_none_kernel(
     with ExitStack() as ctx:
         keep = ctx.enter_context(tc.tile_pool(name="keep", bufs=1))
         ring = ctx.enter_context(tc.tile_pool(name="ring", bufs=4))
-        psum = ctx.enter_context(tc.psum_pool(name="psum", bufs=8))
+        psum = ctx.enter_context(tc.psum_pool(name="psum", bufs=1))
 
-        def bank_tile(name):
-            return psum.tile([P, 512], F32, name=name, tag="bank")
+        def bank_tile(name, bank):
+            return psum.tile([P, 512], F32, name=name, tag="bank%d" % bank)
 
         offs_t = keep.tile([P, S // 16], U16, name="offs_t")
         pos_t = [keep.tile([P, T // 16], U16, name="pos_t%d" % r) for r in range(TOP)]
@@ -52,16 +53,16 @@ def tile_moe_ecr_lin_none_kernel(
             for t0, n in LOAD_CHUNKS:
                 raw[a, t0] = keep.tile([P, 4, n], F32, name="raw", tag="raw%d_%d" % (a, t0))
                 grouped[a, t0] = keep.tile([P, n, 4], BF16, name="grp%d_%d" % (a, t0), align_bytes=64)
-        words = [keep.tile([P, T], U32, name="words%d" % a, align_bytes=64) for a in range(PASSES)]
+        words = [keep.tile([P, T], U32, name="words", tag="words%d" % a, align_bytes=64) for a in range(PASSES)]
         packed = keep.tile([P, WINDOW], U8, name="packed", tag="order", align_bytes=64)
         slot_words = [keep.tile([P, S], U32, name="slotw%d" % a, align_bytes=64) for a in range(PASSES - 1)]
         planes = {}
         for s0, n in HALVES:
             for a in range(PASSES):
                 planes[a, s0] = keep.tile([P, n], U8, name="plane%d_%d" % (a, s0), align_bytes=64)
-        w_t = [keep.tile([P, E, 2 * N], U8, name="w%d" % a, align_bytes=64) for a in range(PASSES)]
+        w_t = [keep.tile([P, E // 2 * PASSES, 2 * N], U8, name="w%d" % h, align_bytes=64) for h in range(2)]
         wsc = keep.tile([P, E * PASSES, N], U8, name="wsc", align_bytes=64)
-        gate_rows = keep.tile([P, TOP, P], F32, name="gate_rows")
+        gate_rows = keep.tile([P, TURNED, P], F32, name="gate_rows")
         ident = keep.tile([P, P], F32, name="ident")
         y = keep.tile([P, S + PAD], F32, name="y")
 
@@ -83,17 +84,16 @@ def tile_moe_ecr_lin_none_kernel(
                 nc.sync.dma_start(offs_t[:], offs)
             if a == 1:
                 nc.sync.dma_start(
-                    out=gate_rows[0 : T // P], in_=gate[:, 0, :].rearrange("r (b c) -> b r c", c=P)
+                    out=gate_rows[0 : T // P], in_=gate[0:TURNED, 0, :].rearrange("r (b c) -> b r c", c=P)
                 )
                 for tile, lst in zip(pos_t, (pos1, pos2, pos3, pos4)):
                     nc.sync.dma_start(tile[:], lst)
-            if a == 2:
-                for r in range(4):
-                    nc.sync.dma_start(out=wsc[r:P:32].bitcast(I32), in_=scale_rows[r].bitcast(I32))
-        for a in range(PASSES):
+        for r in range(4):
+            nc.sync.dma_start(out=wsc[r:P:32].bitcast(I32), in_=scale_rows[r].bitcast(I32))
+        for h in range(2):
             nc.sync.dma_start(
-                out=w_t[a][:].bitcast(I32),
-                in_=w_words[:, a].rearrange("e p c -> p e c").bitcast(I32),
+                out=w_t[h][:].bitcast(I32),
+                in_=w_words[4 * h : 4 * h + 4].rearrange("e a p c -> p (e a) c").bitcast(I32),
             )
 
         def weave(a, t0, lo, hi, on_vector):
@@ -116,6 +116,9 @@ def tile_moe_ecr_lin_none_kernel(
                     cut = n * 5 // 8
                     weave(a, t0, 0, cut, True)
                     weave(a, t0, cut, n, False)
+                elif t0 + n == T:
+                    weave(a, t0, 0, n // 2, True)
+                    weave(a, t0, n // 2, n, False)
                 else:
                     weave(a, t0, 0, n, False)
                 nc.vector.quantize_mx(
@@ -128,13 +131,13 @@ def tile_moe_ecr_lin_none_kernel(
                     gather_words(a, s0, n)
 
         gate_cols = keep.tile(
-            [P, TOP, T // P], F32, name="gate_cols", tag="raw%d_%d" % (PASSES - 1, LOAD_CHUNKS[-1][0])
+            [P, TURNED, T // P], F32, name="gate_cols", tag="raw%d_%d" % (PASSES - 1, LOAD_CHUNKS[-1][0])
         )
-        gbank = bank_tile("gbank")
-        for r in range(TOP):
+        gbank = bank_tile("gbank", 7)
+        for r in range(TURNED):
             nc.tensor.transpose(gbank[:, r * P : (r + 1) * P], gate_rows[:, r, :], ident[:])
         nc.scalar.activation(
-            gate_cols[:], gbank[:].rearrange("p (r c) -> p r c", c=P)[:, :, 0 : T // P], COPY
+            gate_cols[:], gbank[:, 0 : TURNED * P].rearrange("p (r c) -> p r c", c=P)[:, :, 0 : T // P], COPY
         )
 
         for s0, n in HALVES:
@@ -150,7 +153,7 @@ def tile_moe_ecr_lin_none_kernel(
         for s0, n in LAST_PIECES:
             gather_words(PASSES - 1, s0, n)
 
-        acc = [bank_tile("acc%d" % i) for i in range(len(BANKS))]
+        acc = [bank_tile("acc%d" % i, i) for i in range(len(BANKS))]
         for h0, hn in HALVES:
             for a in range(PASSES):
                 for i, (b0, bn) in enumerate(BANKS):
@@ -160,7 +163,7 @@ def tile_moe_ecr_lin_none_kernel(
                         e = s0 // C
                         nc.tensor.matmul_mx(
                             out=acc[i][:, s0 - b0 : s0 - b0 + P],
-                            lhsT=w_t[a][:, e, :].bitcast(FP4X4),
+                            lhsT=w_t[e // 4][:, e % 4 * PASSES + a, :].bitcast(FP4X4),
                             lhsT_scale=wsc[:, e * PASSES + a, :],
                             rhs=slot_words[a][:, s0 : s0 + P].bitcast(FP8X4),
                             rhs_scale=planes[a, h0][:, s0 - h0 : s0 - h0 + P],
@@ -173,55 +176,46 @@ def tile_moe_ecr_lin_none_kernel(
             else:
                 nc.scalar.activation(y[:, b0 : b0 + bn], acc[i][:, 0:bn], COPY)
 
-        def scale_block(dst, src, r, g, on_vector):
-            factor = gate_cols[:, r, g : g + 1]
-            if on_vector:
-                nc.vector.tensor_scalar_mul(dst, src, factor)
-            else:
-                nc.scalar.activation(dst, src, COPY, scale=factor)
-
-        for t0, n in OUT_CHUNKS:
-            last_chunk = t0 + n == T
+        gate_last = keep.tile([P, T], F32, name="gate_last", tag="words%d" % (PASSES - 1), align_bytes=64)
+        nc.sync.dma_start(out=gate_last[:], in_=gate[TURNED])
+        totals = []
+        for c, (t0, n) in enumerate(OUT_CHUNKS):
             blocks = n // P
-            if last_chunk:
-                totals = [bank_tile("total")[:, 0:P] for b in range(blocks)]
-            else:
-                total = bank_tile("total")
-                totals = [total[:, b * P : (b + 1) * P] for b in range(blocks)]
-            for r in range(TOP):
-                very_last = last_chunk and r == TOP - 1
-                picked = ring.tile([P, n], F32, name="picked")
+            total = bank_tile("total", 5 + c)
+            totals.append(total)
+            for r in range(TURNED):
+                picked = keep.tile([P, n], F32, name="picked", tag="raw%d_%d" % (r, LOAD_CHUNKS[c][0]))
                 nc.vector.tensor_copy(
                     picked[:], y[:].indirect(pos_t[r][:, t0 // 16 : (t0 + n) // 16])
                 )
-                if very_last:
-                    turned = [bank_tile("turned")[:, 0:P] for b in range(blocks)]
-                else:
-                    one = bank_tile("turned")
-                    turned = [one[:, b * P : (b + 1) * P] for b in range(blocks)]
+                turned = bank_tile("turned", (c * TURNED + r) % 2)
                 scaled = ring.tile([P, n], F32, name="scaled")
                 for b in range(blocks):
-                    nc.tensor.transpose(turned[b], picked[:, b * P : (b + 1) * P], ident[:])
+                    cols = slice(b * P, (b + 1) * P)
+                    nc.tensor.transpose(turned[:, cols], picked[:, cols], ident[:])
                 for b in range(blocks):
-                    scale_block(
-                        scaled[:, b * P : (b + 1) * P], turned[b], r, t0 // P + b, very_last and b == 1
+                    cols = slice(b * P, (b + 1) * P)
+                    g = t0 // P + b
+                    nc.scalar.activation(
+                        scaled[:, cols], turned[:, cols], COPY, scale=gate_cols[:, r, g : g + 1]
                     )
                 for b in range(blocks):
+                    cols = slice(b * P, (b + 1) * P)
                     nc.tensor.matmul(
-                        totals[b],
-                        scaled[:, b * P : (b + 1) * P],
+                        total[:, cols],
+                        scaled[:, cols],
                         ident[:],
                         is_transpose=True,
-                        start=(r == 0 and (b == 0 or last_chunk)),
-                        stop=(r == TOP - 1 and (b == blocks - 1 or last_chunk)),
+                        start=(r == 0 and b == 0),
+                        stop=(r == TURNED - 1 and b == blocks - 1),
                     )
+        last_term = keep.tile([P, T], F32, name="last_term")
+        nc.vector.tensor_tensor(
+            last_term[:], y[:].indirect(pos_t[TURNED][:]), gate_last[:], mybir.AluOpType.mult
+        )
+        for total, (t0, n) in zip(totals, OUT_CHUNKS):
             staged = ring.tile([P, n], F32, name="staged")
-            if last_chunk:
-                for b in range(blocks):
-                    if b == 1:
-                        nc.scalar.activation(staged[:, b * P : (b + 1) * P], totals[b], COPY)
-                    else:
-                        nc.vector.tensor_copy(staged[:, b * P : (b + 1) * P], totals[b])
-            else:
-                nc.scalar.activation(staged[:], total[:, 0:n], COPY)
+            nc.vector.tensor_tensor(
+                staged[:], total[:, 0:n], last_term[:, t0 : t0 + n], mybir.AluOpType.add
+            )
             nc.sync.dma_start(out=out[:, t0 : t0 + n], in_=staged[:])

@@ -82,12 +82,11 @@ def tile_moe_ecr_lin_none_kernel(
                 nc.sync.dma_start(out=raw[a, t0][:], in_=rows[:, :, t0 : t0 + n])
             if a == 0:
                 nc.sync.dma_start(offs_t[:], offs)
-            if a == 1:
-                nc.sync.dma_start(
-                    out=gate_rows[0 : T // P], in_=gate[0:TURNED, 0, :].rearrange("r (b c) -> b r c", c=P)
-                )
-                for tile, lst in zip(pos_t, (pos1, pos2, pos3, pos4)):
-                    nc.sync.dma_start(tile[:], lst)
+        for tile, lst in zip(pos_t, (pos1, pos2, pos3, pos4)):
+            nc.sync.dma_start(tile[:], lst)
+        nc.sync.dma_start(
+            out=gate_rows[0 : T // P], in_=gate[0:TURNED, 0, :].rearrange("r (b c) -> b r c", c=P)
+        )
         for r in range(4):
             nc.sync.dma_start(out=wsc[r:P:32].bitcast(I32), in_=scale_rows[r].bitcast(I32))
         for h in range(2):
@@ -97,8 +96,8 @@ def tile_moe_ecr_lin_none_kernel(
             )
 
         def weave(a, t0, lo, hi, on_vector):
-            dst = grouped[a, t0][:, lo:hi, :].rearrange("p (c i) t -> p c t i", i=4)
-            src = raw[a, t0][:, :, lo:hi].rearrange("p t (c i) -> p c t i", i=4)
+            dst = grouped[a, t0][:, lo:hi, :].rearrange("p (c i) t -> p c t i", i=2)
+            src = raw[a, t0][:, :, lo:hi].rearrange("p t (c i) -> p c t i", i=2)
             if on_vector:
                 nc.vector.tensor_copy(dst, src)
             else:
@@ -213,9 +212,12 @@ def tile_moe_ecr_lin_none_kernel(
         nc.vector.tensor_tensor(
             last_term[:], y[:].indirect(pos_t[TURNED][:]), gate_last[:], mybir.AluOpType.mult
         )
-        for total, (t0, n) in zip(totals, OUT_CHUNKS):
-            staged = ring.tile([P, n], F32, name="staged")
-            nc.vector.tensor_tensor(
-                staged[:], total[:, 0:n], last_term[:, t0 : t0 + n], mybir.AluOpType.add
-            )
-            nc.sync.dma_start(out=out[:, t0 : t0 + n], in_=staged[:])
+        for total, (c0, cn) in zip(totals, OUT_CHUNKS):
+            cut = cn - P if c0 + cn == T else cn
+            for lo, hi in ((0, cut), (cut, cn)):
+                if hi > lo:
+                    staged = ring.tile([P, hi - lo], F32, name="staged")
+                    nc.vector.tensor_tensor(
+                        staged[:], total[:, lo:hi], last_term[:, c0 + lo : c0 + hi], mybir.AluOpType.add
+                    )
+                    nc.sync.dma_start(out=out[:, c0 + lo : c0 + hi], in_=staged[:])

@@ -54,8 +54,8 @@ def tile_moe_ecr_lin_none_kernel(
                 raw[a, t0] = keep.tile([P, 4, n], F32, name="raw", tag="raw%d_%d" % (a, t0))
                 grouped[a, t0] = keep.tile([P, n, 4], BF16, name="grp%d_%d" % (a, t0), align_bytes=64)
         words = [keep.tile([P, T], U32, name="words", tag="words%d" % a, align_bytes=64) for a in range(PASSES)]
-        packed = keep.tile([P, WINDOW], U8, name="packed", tag="order", align_bytes=64)
-        slot_words = [keep.tile([P, S], U32, name="slotw%d" % a, align_bytes=64) for a in range(PASSES - 1)]
+        packed = keep.tile([P, WINDOW], U8, name="packed", align_bytes=64)
+        slot_words = [keep.tile([P, S], U32, name="slotw%d" % a, align_bytes=64) for a in range(PASSES)]
         planes = {}
         for s0, n in HALVES:
             for a in range(PASSES):
@@ -66,34 +66,38 @@ def tile_moe_ecr_lin_none_kernel(
         ident = keep.tile([P, P], F32, name="ident")
         y = keep.tile([P, S + PAD], F32, name="y")
 
+        nc.vector.memset(wsc[:].bitcast(I32), 0)
         nc.vector.memset(gate_rows[:], 0.0)
         nc.vector.memset(packed[:].bitcast(I32), 0)
-        nc.vector.memset(wsc[:].bitcast(I32), 0)
         for s0, n in HALVES:
             for a in range(1, PASSES):
                 nc.vector.memset(planes[a, s0][:].bitcast(I32), 0)
         nc.vector.memset(y[:, S:], 0.0)
         make_identity(nc, ident[:])
 
-        scale_rows = w_scales.rearrange("e a (q r) n -> r q (e a) n", r=4)
+        scale_rows = w_scales.rearrange("e a q n -> q (e a) n")
         for a in range(PASSES):
             rows = xT[512 * a : 512 * (a + 1), :].rearrange("(p j) t -> p j t", j=4)
             for t0, n in LOAD_CHUNKS:
                 nc.sync.dma_start(out=raw[a, t0][:], in_=rows[:, :, t0 : t0 + n])
             if a == 0:
                 nc.sync.dma_start(offs_t[:], offs)
-        for tile, lst in zip(pos_t, (pos1, pos2, pos3, pos4)):
-            nc.sync.dma_start(tile[:], lst)
-        nc.sync.dma_start(
-            out=gate_rows[0 : T // P], in_=gate[0:TURNED, 0, :].rearrange("r (b c) -> b r c", c=P)
-        )
-        for r in range(4):
-            nc.sync.dma_start(out=wsc[r:P:32].bitcast(I32), in_=scale_rows[r].bitcast(I32))
+            if a == 1:
+                nc.sync.dma_start(
+                    out=gate_rows[0 : T // P], in_=gate[0:TURNED, 0, :].rearrange("r (b c) -> b r c", c=P)
+                )
+            for r in range(4):
+                nc.sync.dma_start(
+                    out=wsc[32 * a + r : 32 * a + r + 1].bitcast(I32),
+                    in_=scale_rows[4 * a + r : 4 * a + r + 1].bitcast(I32),
+                )
         for h in range(2):
             nc.sync.dma_start(
                 out=w_t[h][:].bitcast(I32),
                 in_=w_words[4 * h : 4 * h + 4].rearrange("e a p c -> p (e a) c").bitcast(I32),
             )
+        for tile, lst in zip(pos_t, (pos1, pos2, pos3, pos4)):
+            nc.sync.dma_start(tile[:], lst)
 
         def weave(a, t0, lo, hi, on_vector):
             dst = grouped[a, t0][:, lo:hi, :].rearrange("p (c i) t -> p c t i", i=2)
@@ -148,7 +152,6 @@ def tile_moe_ecr_lin_none_kernel(
                     out=planes[a, s0][0:SHIFT_ROWS].bitcast(I32),
                     in_=planes[0, s0][4 * a : 4 * a + SHIFT_ROWS].bitcast(I32),
                 )
-        slot_words.append(keep.tile([P, S], U32, name="slotw_last", tag="order", align_bytes=64))
         for s0, n in LAST_PIECES:
             gather_words(PASSES - 1, s0, n)
 
@@ -209,9 +212,13 @@ def tile_moe_ecr_lin_none_kernel(
                         stop=(r == TURNED - 1 and b == blocks - 1),
                     )
         last_term = keep.tile([P, T], F32, name="last_term")
-        nc.vector.tensor_tensor(
-            last_term[:], y[:].indirect(pos_t[TURNED][:]), gate_last[:], mybir.AluOpType.mult
-        )
+        for t0, n in ((0, 512), (512, 768)):
+            nc.vector.tensor_tensor(
+                last_term[:, t0 : t0 + n],
+                y[:].indirect(pos_t[TURNED][:, t0 // 16 : (t0 + n) // 16]),
+                gate_last[:, t0 : t0 + n],
+                mybir.AluOpType.mult,
+            )
         for total, (c0, cn) in zip(totals, OUT_CHUNKS):
             cut = cn - P if c0 + cn == T else cn
             for lo, hi in ((0, cut), (cut, cn)):

@@ -28,7 +28,7 @@ PIECES = ((0, 768), (768, 768), (1536, 512))
 LAST_PIECES = ((0, 512), (512, 512), (1024, 512), (1536, 512))
 WINDOW = 1408
 BANKS = ((0, 512), (512, 512), (1024, 512), (1536, 256), (1792, 256))
-OUT_CHUNKS = ((0, 512), (512, 384), (896, 384))
+OUT_CHUNKS = ((0, 384), (384, 384), (768, 512))
 SHIFT_ROWS = 112
 TURNED = TOP - 1
 
@@ -75,29 +75,25 @@ def tile_moe_ecr_lin_none_kernel(
         nc.vector.memset(y[:, S:], 0.0)
         make_identity(nc, ident[:])
 
-        scale_rows = w_scales.rearrange("e a q n -> q (e a) n")
+        scale_rows = w_scales.rearrange("e a (q r) n -> r q (e a) n", r=4)
         for a in range(PASSES):
             rows = xT[512 * a : 512 * (a + 1), :].rearrange("(p j) t -> p j t", j=4)
             for t0, n in LOAD_CHUNKS:
                 nc.sync.dma_start(out=raw[a, t0][:], in_=rows[:, :, t0 : t0 + n])
             if a == 0:
                 nc.sync.dma_start(offs_t[:], offs)
-            if a == 1:
-                nc.sync.dma_start(
-                    out=gate_rows[0 : T // P], in_=gate[0:TURNED, 0, :].rearrange("r (b c) -> b r c", c=P)
-                )
-            for r in range(4):
-                nc.sync.dma_start(
-                    out=wsc[32 * a + r : 32 * a + r + 1].bitcast(I32),
-                    in_=scale_rows[4 * a + r : 4 * a + r + 1].bitcast(I32),
-                )
+        for tile, lst in zip(pos_t, (pos1, pos2, pos3, pos4)):
+            nc.sync.dma_start(tile[:], lst)
+        nc.sync.dma_start(
+            out=gate_rows[0 : T // P], in_=gate[0:TURNED, 0, :].rearrange("r (b c) -> b r c", c=P)
+        )
+        for r in range(4):
+            nc.sync.dma_start(out=wsc[r:P:32].bitcast(I32), in_=scale_rows[r].bitcast(I32))
         for h in range(2):
             nc.sync.dma_start(
                 out=w_t[h][:].bitcast(I32),
                 in_=w_words[4 * h : 4 * h + 4].rearrange("e a p c -> p (e a) c").bitcast(I32),
             )
-        for tile, lst in zip(pos_t, (pos1, pos2, pos3, pos4)):
-            nc.sync.dma_start(tile[:], lst)
 
         def weave(a, t0, lo, hi, on_vector):
             dst = grouped[a, t0][:, lo:hi, :].rearrange("p (c i) t -> p c t i", i=2)
@@ -148,10 +144,12 @@ def tile_moe_ecr_lin_none_kernel(
                 planes[0, s0][:], packed[:].indirect(offs_t[:, s0 // 16 : (s0 + n) // 16])
             )
             for a in range(1, PASSES):
-                nc.sync.dma_start(
-                    out=planes[a, s0][0:SHIFT_ROWS].bitcast(I32),
-                    in_=planes[0, s0][4 * a : 4 * a + SHIFT_ROWS].bitcast(I32),
-                )
+                spans = ((0, SHIFT_ROWS),) if a == PASSES - 1 else ((0, 64), (64, 96), (96, SHIFT_ROWS))
+                for lo, hi in spans:
+                    nc.sync.dma_start(
+                        out=planes[a, s0][lo:hi].bitcast(I32),
+                        in_=planes[0, s0][4 * a + lo : 4 * a + hi].bitcast(I32),
+                    )
         for s0, n in LAST_PIECES:
             gather_words(PASSES - 1, s0, n)
 
@@ -178,19 +176,26 @@ def tile_moe_ecr_lin_none_kernel(
             else:
                 nc.scalar.activation(y[:, b0 : b0 + bn], acc[i][:, 0:bn], COPY)
 
-        gate_last = keep.tile([P, T], F32, name="gate_last", tag="words%d" % (PASSES - 1), align_bytes=64)
-        nc.sync.dma_start(out=gate_last[:], in_=gate[TURNED])
+        tail0, tail_n = OUT_CHUNKS[-1]
+        gate_wide = keep.tile(
+            [P, T + tail_n], F32, name="gate_wide", tag="words%d" % (PASSES - 1), align_bytes=64
+        )
+        nc.sync.dma_start(out=gate_wide[:, 0:T], in_=gate[TOP - 1])
+        nc.sync.dma_start(out=gate_wide[:, T:], in_=gate[TOP - 2, :, tail0:T])
         totals = []
+        unit = 0
         for c, (t0, n) in enumerate(OUT_CHUNKS):
             blocks = n // P
             total = bank_tile("total", 5 + c)
             totals.append(total)
-            for r in range(TURNED):
+            lists = TURNED - 1 if t0 == tail0 else TURNED
+            for r in range(lists):
                 picked = keep.tile([P, n], F32, name="picked", tag="raw%d_%d" % (r, LOAD_CHUNKS[c][0]))
                 nc.vector.tensor_copy(
                     picked[:], y[:].indirect(pos_t[r][:, t0 // 16 : (t0 + n) // 16])
                 )
-                turned = bank_tile("turned", (c * TURNED + r) % 2)
+                turned = bank_tile("turned", unit % 3)
+                unit = unit + 1
                 scaled = ring.tile([P, n], F32, name="scaled")
                 for b in range(blocks):
                     cols = slice(b * P, (b + 1) * P)
@@ -209,22 +214,30 @@ def tile_moe_ecr_lin_none_kernel(
                         ident[:],
                         is_transpose=True,
                         start=(r == 0 and b == 0),
-                        stop=(r == TURNED - 1 and b == blocks - 1),
+                        stop=(r == lists - 1 and b == blocks - 1),
                     )
-        last_term = keep.tile([P, T], F32, name="last_term")
-        for t0, n in ((0, 512), (512, 768)):
+
+        def gated_gather(dst, r, t0, n, factor):
             nc.vector.tensor_tensor(
-                last_term[:, t0 : t0 + n],
-                y[:].indirect(pos_t[TURNED][:, t0 // 16 : (t0 + n) // 16]),
-                gate_last[:, t0 : t0 + n],
+                dst,
+                y[:].indirect(pos_t[r][:, t0 // 16 : (t0 + n) // 16]),
+                factor,
                 mybir.AluOpType.mult,
             )
+
+        term_a = keep.tile([P, tail_n], F32, name="term_a")
+        term_b = keep.tile([P, tail_n], F32, name="term_b")
+        rest = keep.tile([P, T], F32, name="rest")
+        gated_gather(term_a[:], TOP - 2, tail0, tail_n, gate_wide[:, T:])
+        gated_gather(term_b[:], TOP - 1, tail0, tail_n, gate_wide[:, tail0:T])
+        gated_gather(rest[:, 0:tail0], TOP - 1, 0, tail0, gate_wide[:, 0:tail0])
+        nc.vector.tensor_tensor(rest[:, tail0:T], term_a[:], term_b[:], mybir.AluOpType.add)
         for total, (c0, cn) in zip(totals, OUT_CHUNKS):
-            cut = cn - P if c0 + cn == T else cn
+            cut = cn - P if c0 == tail0 else cn
             for lo, hi in ((0, cut), (cut, cn)):
                 if hi > lo:
                     staged = ring.tile([P, hi - lo], F32, name="staged")
                     nc.vector.tensor_tensor(
-                        staged[:], total[:, lo:hi], last_term[:, c0 + lo : c0 + hi], mybir.AluOpType.add
+                        staged[:], total[:, lo:hi], rest[:, c0 + lo : c0 + hi], mybir.AluOpType.add
                     )
                     nc.sync.dma_start(out=out[:, c0 + lo : c0 + hi], in_=staged[:])

from contextlib import ExitStack

import concourse.mybir as mybir
from concourse.masks import make_identity

K, T, E, C, N = 2048, 1280, 8, 256, 128
TOP, PAD = 4, 64
S = E * C
P = 128
PASSES = K // 512

F32 = mybir.dt.float32
BF16 = mybir.dt.bfloat16
I32 = mybir.dt.int32
U32 = mybir.dt.uint32
U16 = mybir.dt.uint16
U8 = mybir.dt.uint8
FP8X4 = mybir.dt.float8_e4m3fn_x4
FP4X4 = mybir.dt.float4_e2m1fn_x4
COPY = mybir.ActivationFunctionType.Copy

FLOPS = 2 * K * S * N
BYTES = K * T * 4 + E * K * N // 2 + E * K * N // 32 + TOP * T * 4 + (S + TOP * T) * 16 + N * T * 4

LOAD_CHUNKS = ((0, 512), (512, 512), (1024, 256))
HALVES = ((0, 1024), (1024, 1024))
PIECES = ((0, 768), (768, 768), (1536, 512))
LAST_PIECES = ((0, 512), (512, 512), (1024, 512), (1536, 512))
WINDOW = 1408
BANKS = ((0, 512), (512, 512), (1024, 512), (1536, 256), (1792, 256))
OUT_CHUNKS = ((0, 384), (384, 384), (768, 512))
SHIFT_ROWS = 112
TURNED = TOP - 1


def tile_moe_ecr_lin_none_kernel(
    tc, xT, w_words, w_scales, gate, offs, pos1, pos2, pos3, pos4, out
):
    nc = tc.nc
    with ExitStack() as ctx:
        keep = ctx.enter_context(tc.tile_pool(name="keep", bufs=1))
        ring = ctx.enter_context(tc.tile_pool(name="ring", bufs=4))
        psum = ctx.enter_context(tc.psum_pool(name="psum", bufs=1))

        def bank_tile(name, bank):
            return psum.tile([P, 512], F32, name=name, tag="bank%d" % bank)

        offs_t = keep.tile([P, S // 16], U16, name="offs_t")
        pos_t = [keep.tile([P, T // 16], U16, name="pos_t%d" % r) for r in range(TOP)]
        raw = {}
        grouped = {}
        for a in range(PASSES):
            for t0, n in LOAD_CHUNKS:
                raw[a, t0] = keep.tile([P, 4, n], F32, name="raw", tag="raw%d_%d" % (a, t0))
                grouped[a, t0] = keep.tile([P, n, 4], BF16, name="grp%d_%d" % (a, t0), align_bytes=64)
        words = [keep.tile([P, T], U32, name="words", tag="words%d" % a, align_bytes=64) for a in range(PASSES)]
        packed = keep.tile([P, WINDOW], U8, name="packed", align_bytes=64)
        slot_words = [keep.tile([P, S], U32, name="slotw%d" % a, align_bytes=64) for a in range(PASSES)]
        planes = {}
        for s0, n in HALVES:
            for a in range(PASSES):
                planes[a, s0] = keep.tile([P, n], U8, name="plane%d_%d" % (a, s0), align_bytes=64)
        w_t = [keep.tile([P, E // 2 * PASSES, 2 * N], U8, name="w%d" % h, align_bytes=64) for h in range(2)]
        wsc = keep.tile([P, E * PASSES, N], U8, name="wsc", align_bytes=64)
        gate_rows = keep.tile([P, TURNED, P], F32, name="gate_rows")
        ident = keep.tile([P, P], F32, name="ident")
        y = keep.tile([P, S + PAD], F32, name="y")

        nc.vector.memset(wsc[:].bitcast(I32), 0)
        nc.vector.memset(gate_rows[:], 0.0)
        nc.vector.memset(packed[:].bitcast(I32), 0)
        for s0, n in HALVES:
            for a in range(1, PASSES):
                nc.vector.memset(planes[a, s0][:].bitcast(I32), 0)
        nc.vector.memset(y[:, S:], 0.0)
        make_identity(nc, ident[:])

        scale_rows = w_scales.rearrange("e a (q r) n -> r q (e a) n", r=4)
        for a in range(PASSES):
            rows = xT[512 * a : 512 * (a + 1), :].rearrange("(p j) t -> p j t", j=4)
            for t0, n in LOAD_CHUNKS:
                nc.sync.dma_start(out=raw[a, t0][:], in_=rows[:, :, t0 : t0 + n])
            if a == 0:
                nc.sync.dma_start(offs_t[:], offs)
        for tile, lst in zip(pos_t, (pos1, pos2, pos3, pos4)):
            nc.sync.dma_start(tile[:], lst)
        nc.sync.dma_start(
            out=gate_rows[0 : T // P], in_=gate[0:TURNED, 0, :].rearrange("r (b c) -> b r c", c=P)
        )
        for r in range(4):
            nc.sync.dma_start(out=wsc[r:P:32].bitcast(I32), in_=scale_rows[r].bitcast(I32))
        for h in range(2):
            nc.sync.dma_start(
                out=w_t[h][:].bitcast(I32),
                in_=w_words[4 * h : 4 * h + 4].rearrange("e a p c -> p (e a) c").bitcast(I32),
            )

        def weave(a, t0, lo, hi, on_vector):
            dst = grouped[a, t0][:, lo:hi, :].rearrange("p (c i) t -> p c t i", i=2)
            src = raw[a, t0][:, :, lo:hi].rearrange("p t (c i) -> p c t i", i=2)
            if on_vector:
                nc.vector.tensor_copy(dst, src)
            else:
                nc.scalar.activation(dst, src, COPY)

        def gather_words(a, s0, n):
            nc.vector.tensor_copy(
                slot_words[a][:, s0 : s0 + n],
                words[a][:].indirect(offs_t[:, s0 // 16 : (s0 + n) // 16]),
            )

        for a in range(PASSES):
            for t0, n in LOAD_CHUNKS:
                if a == 0:
                    cut = n * 5 // 8
                    weave(a, t0, 0, cut, True)
                    weave(a, t0, cut, n, False)
                elif t0 + n == T:
                    weave(a, t0, 0, n // 2, True)
                    weave(a, t0, n // 2, n, False)
                else:
                    weave(a, t0, 0, n, False)
                nc.vector.quantize_mx(
                    out=words[a][:, t0 : t0 + n].bitcast(FP8X4),
                    scales=packed[4 * a : P, t0 : t0 + n],
                    in_=grouped[a, t0][:].rearrange("p w j -> p (w j)"),
                )
            if a < PASSES - 1:
                for s0, n in PIECES:
                    gather_words(a, s0, n)

        gate_cols = keep.tile(
            [P, TURNED, T // P], F32, name="gate_cols", tag="raw%d_%d" % (PASSES - 1, LOAD_CHUNKS[-1][0])
        )
        gbank = bank_tile("gbank", 7)
        for r in range(TURNED):
            nc.tensor.transpose(gbank[:, r * P : (r + 1) * P], gate_rows[:, r, :], ident[:])
        nc.scalar.activation(
            gate_cols[:], gbank[:, 0 : TURNED * P].rearrange("p (r c) -> p r c", c=P)[:, :, 0 : T // P], COPY
        )

        for s0, n in HALVES:
            nc.vector.tensor_copy(
                planes[0, s0][:], packed[:].indirect(offs_t[:, s0 // 16 : (s0 + n) // 16])
            )
            for a in range(1, PASSES):
                spans = ((0, SHIFT_ROWS),) if a == PASSES - 1 else ((0, 64), (64, 96), (96, SHIFT_ROWS))
                for lo, hi in spans:
                    nc.sync.dma_start(
                        out=planes[a, s0][lo:hi].bitcast(I32),
                        in_=planes[0, s0][4 * a + lo : 4 * a + hi].bitcast(I32),
                    )
        for s0, n in LAST_PIECES:
            gather_words(PASSES - 1, s0, n)

        acc = [bank_tile("acc%d" % i, i) for i in range(len(BANKS))]
        for h0, hn in HALVES:
            for a in range(PASSES):
                for i, (b0, bn) in enumerate(BANKS):
                    if not h0 <= b0 < h0 + hn:
                        continue
                    for s0 in range(b0, b0 + bn, P):
                        e = s0 // C
                        nc.tensor.matmul_mx(
                            out=acc[i][:, s0 - b0 : s0 - b0 + P],
                            lhsT=w_t[e // 4][:, e % 4 * PASSES + a, :].bitcast(FP4X4),
                            lhsT_scale=wsc[:, e * PASSES + a, :],
                            rhs=slot_words[a][:, s0 : s0 + P].bitcast(FP8X4),
                            rhs_scale=planes[a, h0][:, s0 - h0 : s0 - h0 + P],
                            start=(a == 0 and s0 == b0),
                            stop=(a == PASSES - 1 and s0 + P == b0 + bn),
                        )
        for i, (b0, bn) in enumerate(BANKS):
            if i == len(BANKS) - 1:
                nc.vector.tensor_copy(y[:, b0 : b0 + bn], acc[i][:, 0:bn])
            else:
                nc.scalar.activation(y[:, b0 : b0 + bn], acc[i][:, 0:bn], COPY)

        tail0, tail_n = OUT_CHUNKS[-1]
        gate_wide = keep.tile(
            [P, T + tail_n], F32, name="gate_wide", tag="words%d" % (PASSES - 1), align_bytes=64
        )
        nc.sync.dma_start(out=gate_wide[:, 0:T], in_=gate[TOP - 1])
        nc.sync.dma_start(out=gate_wide[:, T:], in_=gate[TOP - 2, :, tail0:T])
        totals = []
        unit = 0
        for c, (t0, n) in enumerate(OUT_CHUNKS):
            blocks = n // P
            total = bank_tile("total", 5 + c)
            totals.append(total)
            lists = TURNED - 1 if t0 == tail0 else TURNED
            for r in range(lists):
                picked = keep.tile([P, n], F32, name="picked", tag="raw%d_%d" % (r, LOAD_CHUNKS[c][0]))
                nc.vector.tensor_copy(
                    picked[:], y[:].indirect(pos_t[r][:, t0 // 16 : (t0 + n) // 16])
                )
                turned = bank_tile("turned", unit % 3)
                unit = unit + 1
                scaled = ring.tile([P, n], F32, name="scaled")
                for b in range(blocks):
                    cols = slice(b * P, (b + 1) * P)
                    nc.tensor.transpose(turned[:, cols], picked[:, cols], ident[:])
                for b in range(blocks):
                    cols = slice(b * P, (b + 1) * P)
                    g = t0 // P + b
                    nc.scalar.activation(
                        scaled[:, cols], turned[:, cols], COPY, scale=gate_cols[:, r, g : g + 1]
                    )
                for b in range(blocks):
                    cols = slice(b * P, (b + 1) * P)
                    nc.tensor.matmul(
                        total[:, cols],
                        scaled[:, cols],
                        ident[:],
                        is_transpose=True,
                        start=(r == 0 and b == 0),
                        stop=(r == lists - 1 and b == blocks - 1),
                    )

        def gated_gather(dst, r, t0, n, factor):
            nc.vector.tensor_tensor(
                dst,
                y[:].indirect(pos_t[r][:, t0 // 16 : (t0 + n) // 16]),
                factor,
                mybir.AluOpType.mult,
            )

        term_a = keep.tile([P, tail_n], F32, name="term_a")
        term_b = keep.tile([P, tail_n], F32, name="term_b")
        rest = keep.tile([P, T], F32, name="rest")
        gated_gather(term_a[:], TOP - 2, tail0, tail_n, gate_wide[:, T:])
        gated_gather(term_b[:], TOP - 1, tail0, tail_n, gate_wide[:, tail0:T])
        gated_gather(rest[:, 0:tail0], TOP - 1, 0, tail0, gate_wide[:, 0:tail0])
        nc.vector.tensor_tensor(rest[:, tail0:T], term_a[:], term_b[:], mybir.AluOpType.add)
        for total, (c0, cn) in zip(totals, OUT_CHUNKS):
            cut = cn - P if c0 == tail0 else cn
            for lo, hi in ((0, cut), (cut, cn)):
                if hi > lo:
                    staged = ring.tile([P, hi - lo], F32, name="staged")
                    nc.vector.tensor_tensor(
                        staged[:], total[:, lo:hi], rest[:, c0 + lo : c0 + hi], mybir.AluOpType.add
                    )
                    nc.sync.dma_start(out=out[:, c0 + lo : c0 + hi], in_=staged[:])
